import numpy as np
import ml_dtypes


def mxq(x, axis, fmt="e4m3"):
    dtype, down = {"e4m3": (ml_dtypes.float8_e4m3fn, 7), "e5m2": (ml_dtypes.float8_e5m2, 14)}[fmt]
    v = np.moveaxis(np.asarray(x, np.float32).astype(ml_dtypes.bfloat16).astype(np.float64), axis, -1)
    blocks = v.reshape(v.shape[:-1] + (-1, 32))
    amax = np.abs(blocks).max(-1, keepdims=True)
    byte = np.maximum(np.where(amax > 0, np.frexp(amax)[1] - 1 + 127, 0) - down, 1)
    scale = np.exp2(byte - 127.0)
    codes = (blocks / scale).astype(np.float32).astype(dtype).astype(np.float64)
    return np.moveaxis((codes * scale).reshape(v.shape), -1, axis)


WIDE = False


def mx_kscale(k):
    if not WIDE:
        return np.ones(k)
    levels = np.array([10, -10, 5, -5, 0])
    if k % 512:
        return np.exp2(np.random.permutation(np.resize(levels, k // 32))).repeat(32)
    a = np.empty((k // 512, 16))
    for p in range(k // 512):
        a[p, :8] = np.random.permutation(np.resize(levels, 8))
        for g in range(8):
            far = levels[np.abs(levels - a[p, g]) >= 10]
            a[p, g + 8] = far[np.random.randint(len(far))]
    return np.exp2(a.ravel()).repeat(32)


def f64(x):
    return np.asarray(x).astype(np.float64)


def striped(idx):
    return np.tile(idx.reshape(-1, 16).T, (8, 1)).astype(np.uint16)


def unstriped(offs):
    return offs[:16].T.reshape(-1).astype(np.int64)


def pack_weight(w):
    k, n = w.shape
    w = f64(np.asarray(w, np.float32).astype(ml_dtypes.bfloat16)).reshape(k // 32, 32, n)
    amax = np.abs(w).max(1)
    byte = np.clip(np.where(amax > 0, np.frexp(amax)[1] - 1 + 127 - 7, 1), 1, 254)
    scaled = (w * np.exp2(127.0 - byte)[:, None, :]).reshape(k, n).astype(np.float32)
    words = np.ascontiguousarray(scaled.reshape(k // 512, 128, 4, n).transpose(0, 1, 3, 2)).astype(ml_dtypes.float8_e4m3fn).view(np.uint8)
    return words, np.ascontiguousarray(byte.astype(np.uint8).reshape(k // 512, 16, n))


def unpack_weight(words, scales):
    g, p, n, _ = words.shape
    vals = np.ascontiguousarray(words).view(ml_dtypes.float8_e4m3fn).astype(np.float64) * np.repeat(np.exp2(scales.astype(np.float64) - 127.0), 8, axis=1)[..., None]
    return vals.transpose(0, 1, 3, 2).reshape(g * 512, n)


K, T, S, D, N = 512, 1024, 512, 4, 128
P = 2 ** 7


def setup_inputs():
    n = np.random.standard_normal
    s = mx_kscale(K)[:, None]
    packed_xT = pack_weight(n((K, T)) * s)
    return {
        "x_words": packed_xT[0],
        "x_scales": packed_xT[1],
        "w1": (n((K, N)) / np.sqrt(K) / s).astype(np.float32),
        "comp": (np.tile(np.random.uniform(-0.45, 0.45, (2, 1, S)), (1, P, 1))).astype(np.float32),
        "offs": striped(np.random.permutation(T)[:S]),
        "pos1": striped(np.random.permutation(S)[:S]),
        "pos2": striped(np.random.permutation(S)[:S]),
    }


def reference(x_words, x_scales, w1, comp, offs, pos1, pos2):
    xq = unpack_weight(x_words, x_scales)[:, unstriped(offs)]
    y = mxq(f64(w1), 0, "e4m3").T @ xq
    top = y.reshape(len(y), -1, D).max(axis=2)
    ex = np.exp(y - np.repeat(top, D, axis=1))
    total = ex.reshape(len(ex), -1, D).sum(axis=2)
    prob = ex / np.repeat(total, D, axis=1)
    sup = prob[:, unstriped(pos1)] * f64(comp)[0, :1] + prob[:, unstriped(pos2)] * f64(comp)[1, :1]
    up = prob * (sup + 1.0)
    tot2 = up.reshape(len(up), -1, D).sum(axis=2)
    p2 = (up / np.repeat(tot2, D, axis=1)) ** 2
    return p2.reshape(len(p2), -1, D).sum(axis=2)

@@ -1,0 +1,168 @@
+from contextlib import ExitStack
+
+import concourse.mybir as mybir
+
+F32 = mybir.dt.float32
+BF16 = mybir.dt.bfloat16
+I32 = mybir.dt.int32
+U32 = mybir.dt.uint32
+U16 = mybir.dt.uint16
+U8 = mybir.dt.uint8
+FP8X4 = mybir.dt.float8_e4m3fn_x4
+ALU = mybir.AluOpType
+ACT = mybir.ActivationFunctionType
+AX = mybir.AxisListType
+
+P = 128
+K = 512
+T = 1024
+S = 512
+D = 4
+M = 128
+SOFT = [256,128,128]
+RELAX = [384,128]
+ORDER_A = [["gw",0],["gw",1],["gw",2],["max",0],["max",1],["sub",0],["max",2],["sub",1],["sub",2],["sum",0],["sum",1],["rc",0],["sum",2],["rc",1],["mul",0],["rc",2],["mul",1],["mul",2]]
+ORDER_B = [["g1",0],["g2",0],["g1",1],["sup",0],["g2",1],["up",0],["sup",1],["tot",0],["ars",0],["up",1],["ssq",0],["tot",1],["ars",1],["ssq",1],["res",0],["res",1]]
+
+FLOPS = 2 * K * M * S
+
+
+def spans(widths):
+    starts = [sum(widths[:i]) for i in range(len(widths))]
+    return list(zip(starts, widths))
+
+
+def grouped(ap):
+    return ap.rearrange("p (v d) -> p v d", d=D)
+
+
+def spread(ap, groups):
+    return ap.unsqueeze(2).to_broadcast([P, groups, D])
+
+
+def tile_picked_yrelaxp_sup_p_kernel(tc, x_words, x_scales, w1, comp, offs, pos1, pos2, out):
+    nc = tc.nc
+    with ExitStack() as ctx:
+        keep = ctx.enter_context(tc.tile_pool(name="keep", bufs=1))
+        psum = ctx.enter_context(tc.psum_pool(name="psum", bufs=1))
+
+        offs_t = keep.tile([P, S // 16], U16, name="offs_t")
+        pos1_t = keep.tile([P, S // 16], U16, name="pos1_t")
+        pos2_t = keep.tile([P, S // 16], U16, name="pos2_t")
+        x_sc = keep.tile([P, T], U8, name="x_sc", align_bytes=64)
+        x_wd = keep.tile([P, T], I32, name="x_wd", align_bytes=64)
+        w_raw = keep.tile([P, 4, M], F32, name="w_raw")
+        comp_t = keep.tile([P, 2, S], F32, name="comp_t")
+        warm = keep.tile([P, 8], F32, name="warm")
+        warm_o = keep.tile([P, 8], F32, name="warm_o")
+
+        nc.vector.memset(x_sc[:].bitcast(I32), 0)
+        nc.vector.memset(warm[:], 0.0)
+        nc.sync.dma_start(offs_t[:], offs)
+        for q in range(4):
+            nc.scalar.dma_start(x_sc[32 * q : 32 * q + 4, :].bitcast(I32), x_scales[0, 4 * q : 4 * q + 4, :].bitcast(I32))
+        nc.sync.dma_start(w_raw[:], w1.rearrange("(p j) m -> p j m", j=4))
+        nc.sync.dma_start(x_wd[:], x_words[0].rearrange("p n t -> p (n t)").bitcast(I32))
+        nc.sync.dma_start(pos1_t[:], pos1)
+        nc.sync.dma_start(pos2_t[:], pos2)
+        nc.sync.dma_start(comp_t[:], comp.rearrange("c p s -> p c s"))
+        nc.scalar.activation(warm_o[:], warm[:], ACT.Exp)
+
+        w_bf = keep.tile([P, M, 4], BF16, name="w_bf", align_bytes=64)
+        w_cd = keep.tile([P, M], U32, name="w_cd", align_bytes=64)
+        w_sc = keep.tile([P, M], U8, name="w_sc", align_bytes=64)
+        nc.scalar.copy(w_bf[:], w_raw[:].rearrange("p j m -> p m j"))
+
+        def tiles(name, widths, div=1, dtype=F32):
+            return [keep.tile([P, w // div], dtype, name="%s%d" % (name, h), align_bytes=64) for h, w in enumerate(widths)]
+
+        def entries(lst, a, w):
+            return lst[:, a // 16 : (a + w) // 16]
+
+        g_sc = keep.tile([P, S], U8, name="g_sc", align_bytes=64)
+        g_wd = tiles("g_wd", SOFT, dtype=U32)
+        nc.vector.tensor_copy(g_sc[:], x_sc[:].indirect(offs_t[:]))
+        nc.vector.quantize_mx(out=w_cd[:].bitcast(FP8X4), scales=w_sc[:], in_=w_bf[:].rearrange("p m j -> p (m j)"))
+        y = [psum.tile([P, w], F32, name="y%d" % h) for h, w in enumerate(SOFT)]
+        top, z, ex, total, inv = tiles("top", SOFT, D), tiles("z", SOFT), tiles("ex", SOFT), tiles("total", SOFT, D), tiles("inv", SOFT, D)
+        pair = tiles("pair", SOFT, 2)
+        prob = keep.tile([P, S], F32, name="prob")
+
+        def soft(stage, h):
+            a, w = spans(SOFT)[h]
+            if stage == "gw":
+                nc.vector.tensor_copy(g_wd[h][:], x_wd[:].bitcast(U32).indirect(entries(offs_t, a, w)))
+                for c in range(0, w, 256):
+                    n = min(256, w - c)
+                    nc.tensor.matmul_mx(out=y[h][:, c : c + n], lhsT=w_cd[:].bitcast(FP8X4), lhsT_scale=w_sc[:],
+                                        rhs=g_wd[h][:, c : c + n].bitcast(FP8X4), rhs_scale=g_sc[:, a + c : a + c + n], start=True, stop=True)
+            if stage == "max":
+                nc.vector.tensor_reduce(top[h][:], grouped(y[h][:]), AX.X, ALU.max)
+            if stage == "sub":
+                nc.vector.tensor_tensor(grouped(z[h][:]), grouped(y[h][:]), spread(top[h][:], w // D), ALU.subtract)
+                nc.scalar.activation(ex[h][:], z[h][:], ACT.Exp)
+                if h == len(SOFT) - 1:
+                    nc.scalar.activation(warm_o[:], ex[h][:, 0:8], ACT.Abs_reciprocal_sqrt)
+            if stage == "sum":
+                nc.vector.tensor_reduce(total[h][:], grouped(ex[h][:]), AX.X, ALU.add)
+            if stage == "p1":
+                nc.vector.tensor_tensor(pair[h][:].rearrange("p (v e) -> p v e", e=2), grouped(ex[h][:])[:, :, 0:2], grouped(ex[h][:])[:, :, 2:4], ALU.add)
+            if stage == "p2":
+                nc.vector.tensor_tensor(total[h][:], pair[h][:, 0::2], pair[h][:, 1::2], ALU.add)
+            if stage == "rc":
+                nc.vector.reciprocal(inv[h][:], total[h][:])
+            if stage == "mul":
+                nc.vector.tensor_tensor(grouped(prob[:, a : a + w]), grouped(ex[h][:]), spread(inv[h][:], w // D), ALU.mult)
+            if stage == "gmul":
+                nc.gpsimd.tensor_tensor(grouped(prob[:, a : a + w]), grouped(ex[h][:]), spread(inv[h][:], w // D), ALU.mult)
+
+        for stage, h in ORDER_A:
+            soft(stage, h)
+
+        s1, s2, sup, up, sq = tiles("s1", RELAX), tiles("s2", RELAX), tiles("sup", RELAX), tiles("up", RELAX), tiles("sq", RELAX)
+        tot2, ssq, tsq, inv1, inv2 = tiles("tot2", RELAX, D), tiles("ssq", RELAX, D), tiles("tsq", RELAX, D), tiles("inv1", RELAX, D), tiles("inv2", RELAX, D)
+        pu, pq, half = tiles("pu", RELAX, 2), tiles("pq", RELAX, 2), tiles("half", RELAX, D)
+        res = tiles("res", RELAX, D)
+
+        def finish(h, a, w, left, right):
+            nc.vector.tensor_tensor(res[h][:], left, right, ALU.mult)
+            nc.sync.dma_start(out[:, a // D : (a + w) // D], res[h][:])
+
+        def relax(stage, h):
+            a, w = spans(RELAX)[h]
+            if stage == "g1":
+                nc.vector.tensor_tensor(s1[h][:], prob[:].indirect(entries(pos1_t, a, w)), comp_t[:, 0, a : a + w], ALU.mult)
+            if stage == "g2":
+                nc.vector.tensor_tensor(s2[h][:], prob[:].indirect(entries(pos2_t, a, w)), comp_t[:, 1, a : a + w], ALU.mult)
+            if stage == "sup":
+                nc.vector.scalar_tensor_tensor(sup[h][:], s1[h][:], 1.0, s2[h][:], ALU.add, ALU.add)
+            if stage == "up":
+                nc.vector.tensor_tensor(up[h][:], sup[h][:], prob[:, a : a + w], ALU.mult)
+                nc.scalar.activation(sq[h][:], up[h][:], ACT.Square)
+            if stage == "tot":
+                nc.vector.tensor_reduce(tot2[h][:], grouped(up[h][:]), AX.X, ALU.add)
+            if stage == "t1":
+                nc.vector.tensor_tensor(pu[h][:].rearrange("p (v e) -> p v e", e=2), grouped(up[h][:])[:, :, 0:2], grouped(up[h][:])[:, :, 2:4], ALU.add)
+            if stage == "t2":
+                nc.vector.tensor_tensor(tot2[h][:], pu[h][:, 0::2], pu[h][:, 1::2], ALU.add)
+            if stage == "ars":
+                nc.scalar.activation(tsq[h][:], tot2[h][:], ACT.Square)
+                nc.scalar.activation(inv1[h][:], tsq[h][:], ACT.Abs_reciprocal_sqrt)
+                nc.scalar.activation(inv2[h][:], inv1[h][:], ACT.Square)
+            if stage == "vrc":
+                nc.vector.reciprocal(inv1[h][:], tot2[h][:])
+            if stage == "half":
+                nc.vector.tensor_tensor(half[h][:], ssq[h][:], inv1[h][:], ALU.mult)
+            if stage == "vres":
+                finish(h, a, w, half[h][:], inv1[h][:])
+            if stage == "ssq":
+                nc.vector.tensor_reduce(ssq[h][:], grouped(sq[h][:]), AX.X, ALU.add)
+            if stage == "q1":
+                nc.vector.tensor_tensor(pq[h][:].rearrange("p (v e) -> p v e", e=2), grouped(sq[h][:])[:, :, 0:2], grouped(sq[h][:])[:, :, 2:4], ALU.add)
+            if stage == "q2":
+                nc.vector.tensor_tensor(ssq[h][:], pq[h][:, 0::2], pq[h][:, 1::2], ALU.add)
+            if stage == "res":
+                finish(h, a, w, ssq[h][:], inv2[h][:])
+
+        for stage, h in ORDER_B:
+            relax(stage, h)

@@ -19,10 +19,10 @@ T = 1024
 S = 512
 D = 4
 M = 128
-SOFT = [256,128,128]
-RELAX = [384,128]
-ORDER_A = [["gw",0],["gw",1],["gw",2],["max",0],["max",1],["sub",0],["max",2],["sub",1],["sub",2],["sum",0],["sum",1],["rc",0],["sum",2],["rc",1],["mul",0],["rc",2],["mul",1],["mul",2]]
-ORDER_B = [["g1",0],["g2",0],["g1",1],["sup",0],["g2",1],["up",0],["sup",1],["tot",0],["ars",0],["up",1],["ssq",0],["tot",1],["ars",1],["ssq",1],["res",0],["res",1]]
+SOFT = [128,256,128]
+RELAX = [320,192]
+ORDER_A = [["gw",0],["gw",1],["max",0],["gw",2],["max",1],["sub",0],["max",2],["sub",1],["sum",0],["sub",2],["sum",1],["rc",0],["sum",2],["rc",1],["mul",0],["rc",2],["mul",1],["mul",2]]
+ORDER_B = [["g1",0],["g1",1],["g2",0],["g2",1],["sup",0],["sup",1],["up",0],["up",1],["tot",0],["tot",1],["ars",0],["ars",1],["ssq",0],["ssq",1],["res",0],["res",1]]
 
 FLOPS = 2 * K * M * S
 
@@ -57,11 +57,11 @@ def tile_picked_yrelaxp_sup_p_kernel(tc, x_words, x_scales, w1, comp, offs, pos1
         warm_o = keep.tile([P, 8], F32, name="warm_o")
 
         nc.vector.memset(x_sc[:].bitcast(I32), 0)
-        nc.vector.memset(warm[:], 0.0)
+        nc.gpsimd.memset(warm[:], 0.0)
         nc.sync.dma_start(offs_t[:], offs)
-        for q in range(4):
-            nc.scalar.dma_start(x_sc[32 * q : 32 * q + 4, :].bitcast(I32), x_scales[0, 4 * q : 4 * q + 4, :].bitcast(I32))
         nc.sync.dma_start(w_raw[:], w1.rearrange("(p j) m -> p j m", j=4))
+        for q in range(4):
+            nc.sync.dma_start(x_sc[32 * q : 32 * q + 4, :].bitcast(I32), x_scales[0, 4 * q : 4 * q + 4, :].bitcast(I32))
         nc.sync.dma_start(x_wd[:], x_words[0].rearrange("p n t -> p (n t)").bitcast(I32))
         nc.sync.dma_start(pos1_t[:], pos1)
         nc.sync.dma_start(pos2_t[:], pos2)

@@ -58,8 +58,8 @@ def tile_picked_yrelaxp_sup_p_kernel(tc, x_words, x_scales, w1, comp, offs, pos1
 
         nc.vector.memset(x_sc[:].bitcast(I32), 0)
         nc.gpsimd.memset(warm[:], 0.0)
-        nc.sync.dma_start(offs_t[:], offs)
         nc.sync.dma_start(w_raw[:], w1.rearrange("(p j) m -> p j m", j=4))
+        nc.sync.dma_start(offs_t[:], offs)
         for q in range(4):
             nc.sync.dma_start(x_sc[32 * q : 32 * q + 4, :].bitcast(I32), x_scales[0, 4 * q : 4 * q + 4, :].bitcast(I32))
         nc.sync.dma_start(x_wd[:], x_words[0].rearrange("p n t -> p (n t)").bitcast(I32))
@@ -71,7 +71,7 @@ def tile_picked_yrelaxp_sup_p_kernel(tc, x_words, x_scales, w1, comp, offs, pos1
         w_bf = keep.tile([P, M, 4], BF16, name="w_bf", align_bytes=64)
         w_cd = keep.tile([P, M], U32, name="w_cd", align_bytes=64)
         w_sc = keep.tile([P, M], U8, name="w_sc", align_bytes=64)
-        nc.scalar.copy(w_bf[:], w_raw[:].rearrange("p j m -> p m j"))
+        nc.vector.tensor_copy(w_bf[:], w_raw[:].rearrange("p j m -> p m j"))
 
         def tiles(name, widths, div=1, dtype=F32):
             return [keep.tile([P, w // div], dtype, name="%s%d" % (name, h), align_bytes=64) for h, w in enumerate(widths)]

from contextlib import ExitStack

import concourse.mybir as mybir

F32 = mybir.dt.float32
BF16 = mybir.dt.bfloat16
I32 = mybir.dt.int32
U32 = mybir.dt.uint32
U16 = mybir.dt.uint16
U8 = mybir.dt.uint8
FP8X4 = mybir.dt.float8_e4m3fn_x4
ALU = mybir.AluOpType
ACT = mybir.ActivationFunctionType
AX = mybir.AxisListType

P = 128
K = 512
T = 1024
S = 512
D = 4
M = 128
SOFT = [128,256,128]
RELAX = [320,192]
ORDER_A = [["gw",0],["gw",1],["max",0],["gw",2],["max",1],["sub",0],["max",2],["sub",1],["sum",0],["sub",2],["sum",1],["rc",0],["sum",2],["rc",1],["mul",0],["rc",2],["mul",1],["mul",2]]
ORDER_B = [["g1",0],["g1",1],["g2",0],["g2",1],["sup",0],["sup",1],["up",0],["up",1],["tot",0],["tot",1],["ars",0],["ars",1],["ssq",0],["ssq",1],["res",0],["res",1]]

FLOPS = 2 * K * M * S


def spans(widths):
    starts = [sum(widths[:i]) for i in range(len(widths))]
    return list(zip(starts, widths))


def grouped(ap):
    return ap.rearrange("p (v d) -> p v d", d=D)


def spread(ap, groups):
    return ap.unsqueeze(2).to_broadcast([P, groups, D])


def tile_picked_yrelaxp_sup_p_kernel(tc, x_words, x_scales, w1, comp, offs, pos1, pos2, out):
    nc = tc.nc
    with ExitStack() as ctx:
        keep = ctx.enter_context(tc.tile_pool(name="keep", bufs=1))
        psum = ctx.enter_context(tc.psum_pool(name="psum", bufs=1))

        offs_t = keep.tile([P, S // 16], U16, name="offs_t")
        pos1_t = keep.tile([P, S // 16], U16, name="pos1_t")
        pos2_t = keep.tile([P, S // 16], U16, name="pos2_t")
        x_sc = keep.tile([P, T], U8, name="x_sc", align_bytes=64)
        x_wd = keep.tile([P, T], I32, name="x_wd", align_bytes=64)
        w_raw = keep.tile([P, 4, M], F32, name="w_raw")
        comp_t = keep.tile([P, 2, S], F32, name="comp_t")
        warm = keep.tile([P, 8], F32, name="warm")
        warm_o = keep.tile([P, 8], F32, name="warm_o")

        nc.vector.memset(x_sc[:].bitcast(I32), 0)
        nc.gpsimd.memset(warm[:], 0.0)
        nc.sync.dma_start(w_raw[:], w1.rearrange("(p j) m -> p j m", j=4))
        nc.sync.dma_start(offs_t[:], offs)
        for q in range(4):
            nc.sync.dma_start(x_sc[32 * q : 32 * q + 4, :].bitcast(I32), x_scales[0, 4 * q : 4 * q + 4, :].bitcast(I32))
        nc.sync.dma_start(x_wd[:], x_words[0].rearrange("p n t -> p (n t)").bitcast(I32))
        nc.sync.dma_start(pos1_t[:], pos1)
        nc.sync.dma_start(pos2_t[:], pos2)
        nc.sync.dma_start(comp_t[:], comp.rearrange("c p s -> p c s"))
        nc.scalar.activation(warm_o[:], warm[:], ACT.Exp)

        w_bf = keep.tile([P, M, 4], BF16, name="w_bf", align_bytes=64)
        w_cd = keep.tile([P, M], U32, name="w_cd", align_bytes=64)
        w_sc = keep.tile([P, M], U8, name="w_sc", align_bytes=64)
        nc.vector.tensor_copy(w_bf[:], w_raw[:].rearrange("p j m -> p m j"))

        def tiles(name, widths, div=1, dtype=F32):
            return [keep.tile([P, w // div], dtype, name="%s%d" % (name, h), align_bytes=64) for h, w in enumerate(widths)]

        def entries(lst, a, w):
            return lst[:, a // 16 : (a + w) // 16]

        g_sc = keep.tile([P, S], U8, name="g_sc", align_bytes=64)
        g_wd = tiles("g_wd", SOFT, dtype=U32)
        nc.vector.tensor_copy(g_sc[:], x_sc[:].indirect(offs_t[:]))
        nc.vector.quantize_mx(out=w_cd[:].bitcast(FP8X4), scales=w_sc[:], in_=w_bf[:].rearrange("p m j -> p (m j)"))
        y = [psum.tile([P, w], F32, name="y%d" % h) for h, w in enumerate(SOFT)]
        top, z, ex, total, inv = tiles("top", SOFT, D), tiles("z", SOFT), tiles("ex", SOFT), tiles("total", SOFT, D), tiles("inv", SOFT, D)
        pair = tiles("pair", SOFT, 2)
        prob = keep.tile([P, S], F32, name="prob")

        def soft(stage, h):
            a, w = spans(SOFT)[h]
            if stage == "gw":
                nc.vector.tensor_copy(g_wd[h][:], x_wd[:].bitcast(U32).indirect(entries(offs_t, a, w)))
                for c in range(0, w, 256):
                    n = min(256, w - c)
                    nc.tensor.matmul_mx(out=y[h][:, c : c + n], lhsT=w_cd[:].bitcast(FP8X4), lhsT_scale=w_sc[:],
                                        rhs=g_wd[h][:, c : c + n].bitcast(FP8X4), rhs_scale=g_sc[:, a + c : a + c + n], start=True, stop=True)
            if stage == "max":
                nc.vector.tensor_reduce(top[h][:], grouped(y[h][:]), AX.X, ALU.max)
            if stage == "sub":
                nc.vector.tensor_tensor(grouped(z[h][:]), grouped(y[h][:]), spread(top[h][:], w // D), ALU.subtract)
                nc.scalar.activation(ex[h][:], z[h][:], ACT.Exp)
                if h == len(SOFT) - 1:
                    nc.scalar.activation(warm_o[:], ex[h][:, 0:8], ACT.Abs_reciprocal_sqrt)
            if stage == "sum":
                nc.vector.tensor_reduce(total[h][:], grouped(ex[h][:]), AX.X, ALU.add)
            if stage == "p1":
                nc.vector.tensor_tensor(pair[h][:].rearrange("p (v e) -> p v e", e=2), grouped(ex[h][:])[:, :, 0:2], grouped(ex[h][:])[:, :, 2:4], ALU.add)
            if stage == "p2":
                nc.vector.tensor_tensor(total[h][:], pair[h][:, 0::2], pair[h][:, 1::2], ALU.add)
            if stage == "rc":
                nc.vector.reciprocal(inv[h][:], total[h][:])
            if stage == "mul":
                nc.vector.tensor_tensor(grouped(prob[:, a : a + w]), grouped(ex[h][:]), spread(inv[h][:], w // D), ALU.mult)
            if stage == "gmul":
                nc.gpsimd.tensor_tensor(grouped(prob[:, a : a + w]), grouped(ex[h][:]), spread(inv[h][:], w // D), ALU.mult)

        for stage, h in ORDER_A:
            soft(stage, h)

        s1, s2, sup, up, sq = tiles("s1", RELAX), tiles("s2", RELAX), tiles("sup", RELAX), tiles("up", RELAX), tiles("sq", RELAX)
        tot2, ssq, tsq, inv1, inv2 = tiles("tot2", RELAX, D), tiles("ssq", RELAX, D), tiles("tsq", RELAX, D), tiles("inv1", RELAX, D), tiles("inv2", RELAX, D)
        pu, pq, half = tiles("pu", RELAX, 2), tiles("pq", RELAX, 2), tiles("half", RELAX, D)
        res = tiles("res", RELAX, D)

        def finish(h, a, w, left, right):
            nc.vector.tensor_tensor(res[h][:], left, right, ALU.mult)
            nc.sync.dma_start(out[:, a // D : (a + w) // D], res[h][:])

        def relax(stage, h):
            a, w = spans(RELAX)[h]
            if stage == "g1":
                nc.vector.tensor_tensor(s1[h][:], prob[:].indirect(entries(pos1_t, a, w)), comp_t[:, 0, a : a + w], ALU.mult)
            if stage == "g2":
                nc.vector.tensor_tensor(s2[h][:], prob[:].indirect(entries(pos2_t, a, w)), comp_t[:, 1, a : a + w], ALU.mult)
            if stage == "sup":
                nc.vector.scalar_tensor_tensor(sup[h][:], s1[h][:], 1.0, s2[h][:], ALU.add, ALU.add)
            if stage == "up":
                nc.vector.tensor_tensor(up[h][:], sup[h][:], prob[:, a : a + w], ALU.mult)
                nc.scalar.activation(sq[h][:], up[h][:], ACT.Square)
            if stage == "tot":
                nc.vector.tensor_reduce(tot2[h][:], grouped(up[h][:]), AX.X, ALU.add)
            if stage == "t1":
                nc.vector.tensor_tensor(pu[h][:].rearrange("p (v e) -> p v e", e=2), grouped(up[h][:])[:, :, 0:2], grouped(up[h][:])[:, :, 2:4], ALU.add)
            if stage == "t2":
                nc.vector.tensor_tensor(tot2[h][:], pu[h][:, 0::2], pu[h][:, 1::2], ALU.add)
            if stage == "ars":
                nc.scalar.activation(tsq[h][:], tot2[h][:], ACT.Square)
                nc.scalar.activation(inv1[h][:], tsq[h][:], ACT.Abs_reciprocal_sqrt)
                nc.scalar.activation(inv2[h][:], inv1[h][:], ACT.Square)
            if stage == "vrc":
                nc.vector.reciprocal(inv1[h][:], tot2[h][:])
            if stage == "half":
                nc.vector.tensor_tensor(half[h][:], ssq[h][:], inv1[h][:], ALU.mult)
            if stage == "vres":
                finish(h, a, w, half[h][:], inv1[h][:])
            if stage == "ssq":
                nc.vector.tensor_reduce(ssq[h][:], grouped(sq[h][:]), AX.X, ALU.add)
            if stage == "q1":
                nc.vector.tensor_tensor(pq[h][:].rearrange("p (v e) -> p v e", e=2), grouped(sq[h][:])[:, :, 0:2], grouped(sq[h][:])[:, :, 2:4], ALU.add)
            if stage == "q2":
                nc.vector.tensor_tensor(ssq[h][:], pq[h][:, 0::2], pq[h][:, 1::2], ALU.add)
            if stage == "res":
                finish(h, a, w, ssq[h][:], inv2[h][:])

        for stage, h in ORDER_B:
            relax(stage, h)
